import numpy as np
CORES = [9,13,81,85,89,93,97,101,113,117,121,125]
N = 12
KT, FB, TK = 1, 64, 512
def setup_inputs(rng):
    return {"x": rng.standard_normal((N, 128, KT * TK), dtype=np.float32), "w": rng.standard_normal((N, 128, KT * N * FB), dtype=np.float32)}
def setup_inputs_big(rng):
    d = setup_inputs(rng)
    for k in ("x", "w"): d[k] = (d[k].astype(np.float32) * 1024.0).astype(d[k].dtype)
    return d
def setup_inputs_small(rng):
    d = setup_inputs(rng)
    for k in ("x", "w"): d[k] = (d[k].astype(np.float32) * (1 / 1024.0)).astype(d[k].dtype)
    return d
def setup_inputs_apart(rng):
    d = setup_inputs(rng)
    f = (10.0 ** rng.permutation(np.linspace(-1.5, 1.5, N))).astype(np.float32).reshape(N, 1, 1)
    for k in ("x", "w"): d[k] = (d[k].astype(np.float32) * f).astype(d[k].dtype)
    return d
def reference(x, w):
    X, W = x.astype(np.float64), w.astype(np.float64)
    y = np.zeros((N, FB, N * TK))
    for j in range(N):
        for r in range(N):
            for t in range(KT):
                y[r][:, TK * j:TK * j + TK] += W[j][:, FB * (N * t + r):FB * (N * t + r) + FB].T @ X[j][:, TK * t:TK * t + TK]
    return {"y": y.astype(np.float32 if x.dtype != np.float64 else np.float64)}

@@ -1,0 +1,219 @@
+from concourse.bass import DstId, RemoteDMATransfer
+
+NSIM = 128
+N, FB, TK = 12, 64, 512
+HC = TK // 2
+ORDER = ("X1", "Q1", "X2", "X0", "D2", "own")
+FAR = False
+NSTEP = len(ORDER)
+
+SCRATCH = {
+    "xs": ("sbuf", [128, TK], "float32"),
+    "ws": ("sbuf", [128, N * FB], "float32"),
+    "stage": ("sbuf", [128, 2 * NSTEP * HC], "float32"),
+    "land": ("sbuf", [128, N * HC], "float32"),
+    "relay": ("sbuf", [128, 8 * HC], "float32"),
+}
+for _k in range(NSTEP):
+    SCRATCH["ps%d" % _k] = ("psum", [128, TK], "float32")
+
+SEMAPHORES = (["ldx", "ldw0", "ldw1", "cps", "sent", "sta", "stb"]
+              + ["mm%d" % k for k in range(NSTEP)] + ["cp%d" % k for k in range(NSTEP)]
+              + ["arr%d" % j for j in range(N)] + ["rl%d" % k for k in range(NSTEP)])
+
+
+def _bits(m):
+    return [e for e in range(m.bit_length()) if (m >> e) & 1]
+
+
+def _mask(es):
+    m = 0
+    for e in es:
+        m |= 1 << e
+    return m
+
+
+def _alloc(topo, src, dsts):
+    allowed = [_bits(topo.mask(src, d)) for d in dsts]
+    if len(dsts) == 1:
+        return [allowed[0]]
+    a, b = allowed
+    if len(a) == len(b):
+        return [a[:len(a) // 2], a[len(a) // 2:]]
+    if len(a) < len(b):
+        return [a, [e for e in b if e not in a]]
+    return [[e for e in a if e not in b], b]
+
+
+def _plan(cores, topo):
+    chips = []
+    for c in cores:
+        if topo.chip(c) not in chips:
+            chips.append(topo.chip(c))
+    on = [[r for r, c in enumerate(cores) if topo.chip(c) == ch] for ch in chips]
+    cls0 = [i for i, ch in enumerate(chips) if i == 0 or topo.same_plane(chips[0], ch)]
+    left = [i for i in range(len(chips)) if i not in cls0]
+    part = []
+    for i in cls0:
+        m = [k for k in left if topo.mates(chips[i], chips[k])]
+        part.append(m[0] if m else None)
+        if m:
+            left.remove(m[0])
+    cls1 = [p if p is not None else left.pop(0) for p in part]
+    n = len(cls0)
+    seq = {}
+    for mine, other, sg in ((cls0, cls1, 1), (cls1, cls0, -1)):
+        for pos, i in enumerate(mine):
+            s = []
+            for o in ORDER:
+                if o == "own":
+                    s.append(("own", i))
+                elif o[0] == "X":
+                    s.append(("X", other[(pos + sg * int(o[1:])) % n]))
+                else:
+                    s.append((o[0], mine[(pos + int(o[1:])) % n]))
+            seq[i] = s
+    steps = {}
+    jobs = {}
+    cnt = {}
+    est = {}
+    for i in range(len(chips)):
+        for j in on[i]:
+            cj = cores[j]
+            free = [c for c in range(NSIM) if topo.die(c) == topo.die(cj) and c not in cores]
+            port = [c for c in free if all(topo.may_write(c, d) for d in cores)]
+            owners = [c for c in port if topo.chip(c) == chips[i]]
+            plain = [c for c in free if topo.chip(c) == chips[i] and c not in owners] or owners
+            out = []
+            for k, (kind, d) in enumerate(seq[i]):
+                pair = on[d]
+                if kind == "own":
+                    sib = [r for r in pair if r != j][0]
+                    off = [c for c in cores if topo.chip(c) != chips[i] and topo.may_write(cj, c)][0]
+                    es = [e for e in _bits(topo.mask(cj, cores[sib])) if e not in _bits(topo.mask(cj, off))]
+                    out.append((kind, pair[0], [(pair.index(sib), sib, cores[sib], es, "arr%d" % j, None)]))
+                    cnt[(sib, j)] = len(es)
+                    est[(sib, j)] = k + 1.0
+                    est[(j, j)] = k + 0.3
+                    continue
+                if kind == "D":
+                    eng = _alloc(topo, cj, [cores[r] for r in pair])
+                    out.append((kind, pair[0], [(q, r, cores[r], eng[q], "arr%d" % j, None)
+                                                for q, r in enumerate(pair)]))
+                    for q, r in enumerate(pair):
+                        cnt[(r, j)] = len(eng[q])
+                        est[(r, j)] = k + 1.5
+                    continue
+                lonely = not any(topo.mates(chips[d], ch) for ch in chips)
+                if kind == "X" and FAR and k == 0 and lonely:
+                    via = [c for c in port if topo.mates(topo.chip(c), chips[d])]
+                elif kind in ("X", "P"):
+                    via = owners
+                else:
+                    via = plain[:1]
+                hops = [via[q % len(via)] for q in range(len(pair))]
+                eng = _alloc(topo, cj, hops)
+                tr = []
+                for h in dict.fromkeys(hops):
+                    lst = jobs.setdefault(h, [])
+                    base = sum(len(b[2]) for b in lst)
+                    qs = [q for q in range(len(pair)) if hops[q] == h]
+                    lst.append(("rl%d" % k, sum(len(eng[q]) for q in qs),
+                                [(base + u, pair[q]) for u, q in enumerate(qs)], j))
+                    fw = _alloc(topo, h, [cores[pair[q]] for q in qs])
+                    for u, q in enumerate(qs):
+                        cnt[(pair[q], j)] = len(fw[u])
+                        est[(pair[q], j)] = k + (3.5 if len(qs) > 1 else 3.0)
+                        tr.append((q, pair[q], h, eng[q], "rl%d" % k, base + u))
+                out.append((kind, pair[0], sorted(tr)))
+            steps[j] = out
+    return steps, jobs, cnt, est
+
+
+def _send(g, topo, trs, local_sem):
+    lst = []
+    for dst, es, sem, out_ap, in_ap in trs:
+        rid, pid, _se = topo.addr(dst)
+        lst.append(RemoteDMATransfer(dst_ids=[DstId(rid=rid, pnc=pid)], dma_engine_mask=_mask(es), remote_sem=sem,
+                                     src=in_ap, dst=out_ap))
+    g.remote_dma_fused(lst, local_sem=local_sem)
+    return sum(len(t[1]) for t in trs)
+
+
+def _col(s):
+    return slice(s * HC, (s + 1) * HC)
+
+
+def rank_program(g, core, T, topo):
+    steps, jobs, cnt, est = _plan(T.cores, topo)
+    rank = T.rank_of(core)
+
+    if rank is None:
+        if core not in jobs:
+            return
+        total = 0
+        for sem, count, blocks, j in jobs[core]:
+            g.wait_ge(T.sem[sem], count)
+            eng = _alloc(topo, core, [T.cores[r] for _s, r in blocks])
+            total += _send(g, topo, [(T.cores[r], eng[u], T.sem["arr%d" % j], T.land[:, _col(j)],
+                                      T.relay[:, _col(s)]) for u, (s, r) in enumerate(blocks)], T.sem.sent)
+        g.wait_ge(T.sem.sent, total)
+        return
+
+    my = steps[rank]
+    f0 = my[0][1] * FB
+    g.sync.dma_start(T.xs[:], T.x[:]).then_inc(T.sem.ldx, 16)
+    g.scalar.dma_start(T.ws[:, f0:f0 + 2 * FB], T.w[:, f0:f0 + 2 * FB]).then_inc(T.sem.ldw0, 16)
+    rest = [(a, b) for a, b in ((0, f0), (f0 + 2 * FB, N * FB)) if b > a]
+    for u, (a, b) in enumerate(rest):
+        (g.sync if u == 0 else g.scalar).dma_start(T.ws[:, a:b], T.w[:, a:b]).then_inc(T.sem.ldw1, 16)
+
+    g.tensor.wait_ge(T.sem.ldx, 16)
+    g.tensor.wait_ge(T.sem.ldw0, 16)
+    for k, (kind, r0, tr) in enumerate(my):
+        if k == 1:
+            g.tensor.wait_ge(T.sem.ldw1, 16 * len(rest))
+        g.tensor.matmul(T["ps%d" % k][:], T.ws[:, r0 * FB:(r0 + 2) * FB], T.xs[:], True, True).then_inc(
+            T.sem["mm%d" % k], 1)
+
+    top, bot = (slice(HC, TK), slice(0, HC)) if rank % 2 == 0 else (slice(0, HC), slice(HC, TK))
+    for k, (kind, r0, tr) in enumerate(my):
+        ps = T["ps%d" % k]
+        g.vector.wait_ge(T.sem["mm%d" % k], 1)
+        for q, r, hop, es, sem, slot in tr:
+            rows = slice(q * FB, (q + 1) * FB)
+            g.vector.tensor_copy(T.stage[0:FB, _col(2 * k + q)], ps[rows, top]).then_inc(T.sem["cp%d" % k], 1)
+            g.vector.tensor_copy(T.stage[FB:2 * FB, _col(2 * k + q)], ps[rows, bot]).then_inc(T.sem["cp%d" % k], 1)
+        if kind == "own":
+            rows = slice((rank - r0) * FB, (rank - r0 + 1) * FB)
+            g.vector.tensor_copy(T.land[0:FB, _col(rank)], ps[rows, top]).then_inc(T.sem.cps, 1)
+            g.vector.tensor_copy(T.land[FB:2 * FB, _col(rank)], ps[rows, bot]).then_inc(T.sem.cps, 1)
+
+    total = 0
+    for k, (kind, r0, tr) in enumerate(my):
+        g.wait_ge(T.sem["cp%d" % k], 2 * len(tr))
+        total += _send(g, topo, [(hop, es, T.sem[sem],
+                                  T.land[:, _col(rank)] if slot is None else T.relay[:, _col(slot)],
+                                  T.stage[:, _col(2 * k + q)]) for q, r, hop, es, sem, slot in tr], T.sem.sent)
+    g.wait_ge(T.sem.sent, total)
+
+    st = []
+    for c in range(N // 2):
+        st.append((0, 2 * c, 2, 2 * TK * c + HC))
+    for c in range(N // 2 - 1):
+        st.append((FB, 2 * c + 1, 2, 2 * TK * c + 3 * HC))
+    st.append((FB, 0, 1, 0))
+    st.append((FB, N - 1, 1, N * TK - HC))
+    st.sort(key=lambda s: (max(est[(rank, j)] for j in range(s[1], s[1] + s[2])), s[1]))
+    nq = [0, 0]
+    for u, (p0, slot, ns, col) in enumerate(st):
+        qu, sem = ((g.sync, T.sem.sta), (g.scalar, T.sem.stb))[u % 2]
+        for j in range(slot, slot + ns):
+            if j == rank:
+                qu.wait_ge(T.sem.cps, 2)
+            else:
+                qu.wait_ge(T.sem["arr%d" % j], cnt[(rank, j)])
+        qu.dma_start(T.y[:, col:col + ns * HC], T.land[p0:p0 + FB, slot * HC:(slot + ns) * HC]).then_inc(sem, 16)
+        nq[u % 2] += 16
+    g.sync.wait_ge(T.sem.sta, nq[0])
+    g.scalar.wait_ge(T.sem.stb, nq[1])

@@ -3,12 +3,12 @@ from concourse.bass import DstId, RemoteDMATransfer
 NSIM = 128
 N, FB, TK = 12, 64, 512
 HC = TK // 2
-ORDER = ("X1", "Q1", "X2", "X0", "D2", "own")
-FAR = False
+ORDER = ("C1", "X1", "X2", "X0", "D2", "own")
+ORDER_LONE = ("C1", "X1", "F0", "x2", "D2", "own")
 NSTEP = len(ORDER)
 
 SCRATCH = {
-    "xs": ("sbuf", [128, TK], "float32"),
+    "xw": ("sbuf", [128, TK + 2 * FB], "float32"),
     "ws": ("sbuf", [128, N * FB], "float32"),
     "stage": ("sbuf", [128, 2 * NSTEP * HC], "float32"),
     "land": ("sbuf", [128, N * HC], "float32"),
@@ -17,7 +17,7 @@ SCRATCH = {
 for _k in range(NSTEP):
     SCRATCH["ps%d" % _k] = ("psum", [128, TK], "float32")
 
-SEMAPHORES = (["ldx", "ldw0", "ldw1", "cps", "sent", "sta", "stb"]
+SEMAPHORES = (["ldx", "ldc", "ldw0", "ldw1", "cps", "sent", "sta", "stb"]
               + ["mm%d" % k for k in range(NSTEP)] + ["cp%d" % k for k in range(NSTEP)]
               + ["arr%d" % j for j in range(N)] + ["rl%d" % k for k in range(NSTEP)])
 
@@ -64,12 +64,13 @@ def _plan(cores, topo):
     seq = {}
     for mine, other, sg in ((cls0, cls1, 1), (cls1, cls0, -1)):
         for pos, i in enumerate(mine):
+            lone = not any(topo.mates(chips[i], ch) for ch in chips)
             s = []
-            for o in ORDER:
+            for o in (ORDER_LONE if lone else ORDER):
                 if o == "own":
                     s.append(("own", i))
-                elif o[0] == "X":
-                    s.append(("X", other[(pos + sg * int(o[1:])) % n]))
+                elif o[0] in "XxF":
+                    s.append((o[0], other[(pos + sg * int(o[1:])) % n]))
                 else:
                     s.append((o[0], mine[(pos + int(o[1:])) % n]))
             seq[i] = s
@@ -84,17 +85,29 @@ def _plan(cores, topo):
             port = [c for c in free if all(topo.may_write(c, d) for d in cores)]
             owners = [c for c in port if topo.chip(c) == chips[i]]
             plain = [c for c in free if topo.chip(c) == chips[i] and c not in owners] or owners
+            off = [c for c in cores if topo.chip(c) != chips[i] and topo.may_write(cj, c)][0]
+            stay = [e for e in _bits(topo.mask(cj, owners[0])) if e not in _bits(topo.mask(cj, off))]
             out = []
+            t = 0
             for k, (kind, d) in enumerate(seq[i]):
                 pair = on[d]
+                if kind == "C":
+                    h = plain[0]
+                    es = _bits(topo.mask(cj, h))
+                    out.append((kind, pair[0], [(0, None, h, es, "rl%d" % k, None)]))
+                    jobs.setdefault(h, []).append(("rl%d" % k, len(es), list(enumerate(pair)), j, True))
+                    fw = _alloc(topo, h, [cores[r] for r in pair])
+                    for u, r in enumerate(pair):
+                        cnt[(r, j)] = len(fw[u])
+                        est[(r, j)] = 3.5
+                    continue
+                t += 1
                 if kind == "own":
                     sib = [r for r in pair if r != j][0]
-                    off = [c for c in cores if topo.chip(c) != chips[i] and topo.may_write(cj, c)][0]
-                    es = [e for e in _bits(topo.mask(cj, cores[sib])) if e not in _bits(topo.mask(cj, off))]
-                    out.append((kind, pair[0], [(pair.index(sib), sib, cores[sib], es, "arr%d" % j, None)]))
-                    cnt[(sib, j)] = len(es)
-                    est[(sib, j)] = k + 1.0
-                    est[(j, j)] = k + 0.3
+                    out.append((kind, pair[0], [(pair.index(sib), sib, cores[sib], stay, "arr%d" % j, None)]))
+                    cnt[(sib, j)] = len(stay)
+                    est[(sib, j)] = t
+                    est[(j, j)] = t - 0.7
                     continue
                 if kind == "D":
                     eng = _alloc(topo, cj, [cores[r] for r in pair])
@@ -102,28 +115,29 @@ def _plan(cores, topo):
                                                 for q, r in enumerate(pair)]))
                     for q, r in enumerate(pair):
                         cnt[(r, j)] = len(eng[q])
-                        est[(r, j)] = k + 1.5
+                        est[(r, j)] = t + 0.5
                     continue
-                lonely = not any(topo.mates(chips[d], ch) for ch in chips)
-                if kind == "X" and FAR and k == 0 and lonely:
+                if kind == "F":
                     via = [c for c in port if topo.mates(topo.chip(c), chips[d])]
-                elif kind in ("X", "P"):
+                elif kind in ("X", "x", "P"):
                     via = owners
                 else:
                     via = plain[:1]
                 hops = [via[q % len(via)] for q in range(len(pair))]
                 eng = _alloc(topo, cj, hops)
+                if kind == "x":
+                    eng = [stay[:len(stay) // 2], stay[len(stay) // 2:]]
                 tr = []
                 for h in dict.fromkeys(hops):
                     lst = jobs.setdefault(h, [])
                     base = sum(len(b[2]) for b in lst)
                     qs = [q for q in range(len(pair)) if hops[q] == h]
                     lst.append(("rl%d" % k, sum(len(eng[q]) for q in qs),
-                                [(base + u, pair[q]) for u, q in enumerate(qs)], j))
+                                [(base + u, pair[q]) for u, q in enumerate(qs)], j, False))
                     fw = _alloc(topo, h, [cores[pair[q]] for q in qs])
                     for u, q in enumerate(qs):
                         cnt[(pair[q], j)] = len(fw[u])
-                        est[(pair[q], j)] = k + (3.5 if len(qs) > 1 else 3.0)
+                        est[(pair[q], j)] = t + (3.0 if kind == "F" else 2.0)
                         tr.append((q, pair[q], h, eng[q], "rl%d" % k, base + u))
                 out.append((kind, pair[0], sorted(tr)))
             steps[j] = out
@@ -144,6 +158,17 @@ def _col(s):
     return slice(s * HC, (s + 1) * HC)
 
 
+def _halves(j):
+    return (slice(HC, TK), slice(0, HC)) if j % 2 == 0 else (slice(0, HC), slice(HC, TK))
+
+
+def _unload(g, T, ps, q, j, out, cols, sem):
+    top, bot = _halves(j)
+    rows = slice(q * FB, (q + 1) * FB)
+    g.vector.tensor_copy(out[0:FB, cols], ps[rows, top]).then_inc(sem, 1)
+    g.vector.tensor_copy(out[FB:2 * FB, cols], ps[rows, bot]).then_inc(sem, 1)
+
+
 def rank_program(g, core, T, topo):
     steps, jobs, cnt, est = _plan(T.cores, topo)
     rank = T.rank_of(core)
@@ -152,45 +177,71 @@ def rank_program(g, core, T, topo):
         if core not in jobs:
             return
         total = 0
-        for sem, count, blocks, j in jobs[core]:
-            g.wait_ge(T.sem[sem], count)
+        for sem, count, blocks, j, computes in jobs[core]:
+            src = T.relay
+            if computes:
+                g.tensor.wait_ge(T.sem[sem], count)
+                g.tensor.matmul(T.ps0[:], T.xw[:, TK:TK + 2 * FB], T.xw[:, 0:TK], True, True).then_inc(T.sem.mm0, 1)
+                g.vector.wait_ge(T.sem.mm0, 1)
+                for s, r in blocks:
+                    _unload(g, T, T.ps0, s, j, T.stage, _col(s), T.sem.cp0)
+                g.wait_ge(T.sem.cp0, 2 * len(blocks))
+                src = T.stage
+            else:
+                g.wait_ge(T.sem[sem], count)
             eng = _alloc(topo, core, [T.cores[r] for _s, r in blocks])
             total += _send(g, topo, [(T.cores[r], eng[u], T.sem["arr%d" % j], T.land[:, _col(j)],
-                                      T.relay[:, _col(s)]) for u, (s, r) in enumerate(blocks)], T.sem.sent)
+                                      src[:, _col(s)]) for u, (s, r) in enumerate(blocks)], T.sem.sent)
         g.wait_ge(T.sem.sent, total)
         return
 
     my = steps[rank]
-    f0 = my[0][1] * FB
-    g.sync.dma_start(T.xs[:], T.x[:]).then_inc(T.sem.ldx, 16)
+    mats = [s for s in my if s[0] != "C"]
+    g.sync.dma_start(T.xw[:, 0:TK], T.x[:]).then_inc(T.sem.ldx, 16)
+    taken = [mats[0][1] * FB]
+    for kind, r0, tr in my:
+        if kind == "C":
+            g.scalar.dma_start(T.xw[:, TK:TK + 2 * FB], T.w[:, r0 * FB:(r0 + 2) * FB]).then_inc(T.sem.ldc, 16)
+            taken.append(r0 * FB)
+    f0 = taken[0]
     g.scalar.dma_start(T.ws[:, f0:f0 + 2 * FB], T.w[:, f0:f0 + 2 * FB]).then_inc(T.sem.ldw0, 16)
-    rest = [(a, b) for a, b in ((0, f0), (f0 + 2 * FB, N * FB)) if b > a]
+    rest, a = [], 0
+    for s in sorted(taken) + [N * FB]:
+        if s > a:
+            rest.append((a, s))
+        a = s + 2 * FB
     for u, (a, b) in enumerate(rest):
-        (g.sync if u == 0 else g.scalar).dma_start(T.ws[:, a:b], T.w[:, a:b]).then_inc(T.sem.ldw1, 16)
+        (g.sync if u % 2 == 0 else g.scalar).dma_start(T.ws[:, a:b], T.w[:, a:b]).then_inc(T.sem.ldw1, 16)
 
     g.tensor.wait_ge(T.sem.ldx, 16)
     g.tensor.wait_ge(T.sem.ldw0, 16)
+    first = True
     for k, (kind, r0, tr) in enumerate(my):
-        if k == 1:
+        if kind == "C":
+            continue
+        if not first and rest:
             g.tensor.wait_ge(T.sem.ldw1, 16 * len(rest))
-        g.tensor.matmul(T["ps%d" % k][:], T.ws[:, r0 * FB:(r0 + 2) * FB], T.xs[:], True, True).then_inc(
+            rest = []
+        first = False
+        g.tensor.matmul(T["ps%d" % k][:], T.ws[:, r0 * FB:(r0 + 2) * FB], T.xw[:, 0:TK], True, True).then_inc(
             T.sem["mm%d" % k], 1)
 
-    top, bot = (slice(HC, TK), slice(0, HC)) if rank % 2 == 0 else (slice(0, HC), slice(HC, TK))
     for k, (kind, r0, tr) in enumerate(my):
-        ps = T["ps%d" % k]
+        if kind == "C":
+            continue
         g.vector.wait_ge(T.sem["mm%d" % k], 1)
         for q, r, hop, es, sem, slot in tr:
-            rows = slice(q * FB, (q + 1) * FB)
-            g.vector.tensor_copy(T.stage[0:FB, _col(2 * k + q)], ps[rows, top]).then_inc(T.sem["cp%d" % k], 1)
-            g.vector.tensor_copy(T.stage[FB:2 * FB, _col(2 * k + q)], ps[rows, bot]).then_inc(T.sem["cp%d" % k], 1)
+            _unload(g, T, T["ps%d" % k], q, rank, T.stage, _col(2 * k + q), T.sem["cp%d" % k])
         if kind == "own":
-            rows = slice((rank - r0) * FB, (rank - r0 + 1) * FB)
-            g.vector.tensor_copy(T.land[0:FB, _col(rank)], ps[rows, top]).then_inc(T.sem.cps, 1)
-            g.vector.tensor_copy(T.land[FB:2 * FB, _col(rank)], ps[rows, bot]).then_inc(T.sem.cps, 1)
+            _unload(g, T, T["ps%d" % k], rank - r0, rank, T.land, _col(rank), T.sem.cps)
 
     total = 0
     for k, (kind, r0, tr) in enumerate(my):
+        if kind == "C":
+            g.wait_ge(T.sem.ldx, 16)
+            g.wait_ge(T.sem.ldc, 16)
+            total += _send(g, topo, [(tr[0][2], tr[0][3], T.sem[tr[0][4]], T.xw[:], T.xw[:])], T.sem.sent)
+            continue
         g.wait_ge(T.sem["cp%d" % k], 2 * len(tr))
         total += _send(g, topo, [(hop, es, T.sem[sem],
                                   T.land[:, _col(rank)] if slot is None else T.relay[:, _col(slot)],

@@ -3,23 +3,26 @@ from concourse.bass import DstId, RemoteDMATransfer
 NSIM = 128
 N, FB, TK = 12, 64, 512
 HC = TK // 2
-ORDER = ("C1", "X1", "X2", "X0", "D2", "own")
-ORDER_LONE = ("C1", "X1", "F0", "x2", "D2", "own")
-NSTEP = len(ORDER)
+W2 = 2 * FB
+XO = 2 * W2
+NB = 6
 
 SCRATCH = {
-    "xw": ("sbuf", [128, TK + 2 * FB], "float32"),
+    "xw": ("sbuf", [128, XO + TK + W2], "float32"),
     "ws": ("sbuf", [128, N * FB], "float32"),
-    "stage": ("sbuf", [128, 2 * NSTEP * HC], "float32"),
+    "bun": ("sbuf", [128, TK + 2 * W2], "float32"),
+    "stage": ("sbuf", [128, NB * HC], "float32"),
     "land": ("sbuf", [128, N * HC], "float32"),
-    "relay": ("sbuf", [128, 8 * HC], "float32"),
+    "relay": ("sbuf", [128, 3 * HC], "float32"),
 }
-for _k in range(NSTEP):
+for _k in range(NB):
     SCRATCH["ps%d" % _k] = ("psum", [128, TK], "float32")
 
-SEMAPHORES = (["ldx", "ldc", "ldw0", "ldw1", "cps", "sent", "sta", "stb"]
-              + ["mm%d" % k for k in range(NSTEP)] + ["cp%d" % k for k in range(NSTEP)]
-              + ["arr%d" % j for j in range(N)] + ["rl%d" % k for k in range(NSTEP)])
+SEMAPHORES = (["ldx", "lb", "ldc", "lw0", "lw1", "lw2", "cps", "sent", "sta", "stb", "bp0", "bp1", "cf"]
+              + ["mm%d" % k for k in range(NB)] + ["cp%d" % k for k in range(3)]
+              + ["arr%d" % j for j in range(N)] + ["rl%d" % j for j in range(N)] + ["rx%d" % u for u in range(3)])
+
+LAYOUT = ((XO, 0), (0, TK))
 
 
 def _bits(m):
@@ -33,115 +36,124 @@ def _mask(es):
     return m
 
 
-def _alloc(topo, src, dsts):
-    allowed = [_bits(topo.mask(src, d)) for d in dsts]
-    if len(dsts) == 1:
-        return [allowed[0]]
-    a, b = allowed
-    if len(a) == len(b):
-        return [a[:len(a) // 2], a[len(a) // 2:]]
-    if len(a) < len(b):
-        return [a, [e for e in b if e not in a]]
-    return [[e for e in a if e not in b], b]
-
-
 def _plan(cores, topo):
-    chips = []
-    for c in cores:
-        if topo.chip(c) not in chips:
-            chips.append(topo.chip(c))
-    on = [[r for r, c in enumerate(cores) if topo.chip(c) == ch] for ch in chips]
-    cls0 = [i for i, ch in enumerate(chips) if i == 0 or topo.same_plane(chips[0], ch)]
-    left = [i for i in range(len(chips)) if i not in cls0]
-    part = []
-    for i in cls0:
-        m = [k for k in left if topo.mates(chips[i], chips[k])]
-        part.append(m[0] if m else None)
-        if m:
-            left.remove(m[0])
-    cls1 = [p if p is not None else left.pop(0) for p in part]
-    n = len(cls0)
-    seq = {}
-    for mine, other, sg in ((cls0, cls1, 1), (cls1, cls0, -1)):
-        for pos, i in enumerate(mine):
-            lone = not any(topo.mates(chips[i], ch) for ch in chips)
-            s = []
-            for o in (ORDER_LONE if lone else ORDER):
-                if o == "own":
-                    s.append(("own", i))
-                elif o[0] in "XxF":
-                    s.append((o[0], other[(pos + sg * int(o[1:])) % n]))
-                else:
-                    s.append((o[0], mine[(pos + int(o[1:])) % n]))
-            seq[i] = s
-    steps = {}
-    jobs = {}
-    cnt = {}
-    est = {}
-    for i in range(len(chips)):
-        for j in on[i]:
-            cj = cores[j]
-            free = [c for c in range(NSIM) if topo.die(c) == topo.die(cj) and c not in cores]
-            port = [c for c in free if all(topo.may_write(c, d) for d in cores)]
-            owners = [c for c in port if topo.chip(c) == chips[i]]
-            plain = [c for c in free if topo.chip(c) == chips[i] and c not in owners] or owners
-            off = [c for c in cores if topo.chip(c) != chips[i] and topo.may_write(cj, c)][0]
-            stay = [e for e in _bits(topo.mask(cj, owners[0])) if e not in _bits(topo.mask(cj, off))]
-            out = []
-            t = 0
-            for k, (kind, d) in enumerate(seq[i]):
-                pair = on[d]
-                if kind == "C":
-                    h = plain[0]
-                    es = _bits(topo.mask(cj, h))
-                    out.append((kind, pair[0], [(0, None, h, es, "rl%d" % k, None)]))
-                    jobs.setdefault(h, []).append(("rl%d" % k, len(es), list(enumerate(pair)), j, True))
-                    fw = _alloc(topo, h, [cores[r] for r in pair])
-                    for u, r in enumerate(pair):
-                        cnt[(r, j)] = len(fw[u])
-                        est[(r, j)] = 3.5
-                    continue
-                t += 1
-                if kind == "own":
-                    sib = [r for r in pair if r != j][0]
-                    out.append((kind, pair[0], [(pair.index(sib), sib, cores[sib], stay, "arr%d" % j, None)]))
-                    cnt[(sib, j)] = len(stay)
-                    est[(sib, j)] = t
-                    est[(j, j)] = t - 0.7
-                    continue
-                if kind == "D":
-                    eng = _alloc(topo, cj, [cores[r] for r in pair])
-                    out.append((kind, pair[0], [(q, r, cores[r], eng[q], "arr%d" % j, None)
-                                                for q, r in enumerate(pair)]))
-                    for q, r in enumerate(pair):
-                        cnt[(r, j)] = len(eng[q])
-                        est[(r, j)] = t + 0.5
-                    continue
-                if kind == "F":
-                    via = [c for c in port if topo.mates(topo.chip(c), chips[d])]
-                elif kind in ("X", "x", "P"):
-                    via = owners
-                else:
-                    via = plain[:1]
-                hops = [via[q % len(via)] for q in range(len(pair))]
-                eng = _alloc(topo, cj, hops)
-                if kind == "x":
-                    eng = [stay[:len(stay) // 2], stay[len(stay) // 2:]]
+    allchips = sorted({topo.chip(c) for c in range(NSIM)})
+    chips = list(dict.fromkeys(topo.chip(c) for c in cores))
+    on = {ch: [r for r, c in enumerate(cores) if topo.chip(c) == ch] for ch in chips}
+    gm = {ch: ([o for o in chips if topo.mates(ch, o)] or [None])[0] for ch in chips}
+    am = {ch: [o for o in allchips if topo.mates(ch, o)][0] for ch in chips}
+
+    def free(ch, d):
+        return [c for c in range(NSIM) if topo.chip(c) == ch and topo.die(c) == d and c not in cores]
+
+    def owners(ch, d):
+        return [c for c in free(ch, d) if all(topo.may_write(c, t) for t in cores)]
+
+    def eng(c):
+        near = [o for o in range(NSIM) if o != c and topo.chip(o) == topo.chip(c)][0]
+        far = [o for o in range(NSIM) if topo.chip(o) != topo.chip(c)][0]
+        of = _bits(topo.mask(c, far))
+        return of, [e for e in _bits(topo.mask(c, near)) if e not in of]
+
+    L, MM, CP, ON, OFF = 2.2, 1.9, 0.5, 2.3, 3.0
+    src, jobs, cnt, est, nb, nf = {}, {}, {}, {}, {}, {}
+    for j, cj in enumerate(cores):
+        a, d = topo.chip(cj), topo.die(cj)
+        off, stay = eng(cj)
+        mine = owners(a, d)
+        bund, cst, units = [], None, []
+        for b in chips:
+            if b == a:
+                continue
+            if gm[b] is not None and gm[b] != a:
+                if topo.same_plane(a, b):
+                    bund.append(b)
+            elif gm[b] == a:
+                units.insert(0, ("X", b))
+            elif topo.same_plane(a, b):
+                cst = b
+            elif gm[a] is None:
+                units.append(("X", b))
+            else:
+                units.append(("F", b))
+        for t in bund[1:]:
+            cst = t
+            units.insert(0, ("X", gm[t]))
+        units.append(("own", a))
+
+        t = bund[0]
+        if gm[a] is None:
+            idle = [c for c in allchips if topo.same_plane(a, c) and c not in chips
+                    and not any(topo.mates(c, o) for o in chips)][0]
+            h = owners(idle, d)[0]
+            hoff, hstay = eng(h)
+            ways = ((gm[t], hoff, OFF), (t, hoff, OFF + 2.0))
+        else:
+            k = nb.get((t, d), 0)
+            nb[(t, d)] = k + 1
+            h = owners(t, d)[k]
+            hoff, hstay = eng(h)
+            ways = ((gm[t], hoff, OFF), (t, hstay, ON))
+        two = sorted((t, gm[t]), key=lambda ch: on[ch][0])
+        us = []
+        for u, (ch, ee, hop) in enumerate(ways):
+            half = len(ee) // 2
+            us.append((on[ch], two.index(ch) * W2, [ee[:half], ee[half:]]))
+            for r in on[ch]:
+                cnt[(r, j)] = half
+                est[(r, j)] = L + OFF + 1.5 + (u + 1) * MM / 2 + CP + hop
+        jobs.setdefault(h, []).append(("K", j, [("bp0", len(off)), ("bp1", len(off))], 0, us))
+        pb = (h, off, [on[ch][0] for ch in two])
+
+        h = [c for c in free(a, d) if c not in mine][0]
+        hoff, _hs = eng(h)
+        half = len(hoff) // 2
+        jobs.setdefault(h, []).append(("K", j, [("cf", len(stay)), None], 1, [(on[cst], 0, [hoff[:half], hoff[half:]])]))
+        for r in on[cst]:
+            cnt[(r, j)] = half
+            est[(r, j)] = L + ON + MM + CP + OFF
+        pc = (h, stay, on[cst][0])
+
+        pu = []
+        for u, (kind, b) in enumerate(units):
+            ready = L + (u + 1) * MM + CP
+            pair = on[b]
+            if kind == "own":
+                sib = [r for r in pair if r != j][0]
+                pu.append((kind, pair[0], [(cores[sib], stay, "arr%d" % j, "land", j, 1, 2 * u + pair.index(sib))]))
+                cnt[(sib, j)] = len(stay)
+                est[(sib, j)] = ready + ON
+                est[(j, j)] = ready
+            elif kind == "X":
                 tr = []
-                for h in dict.fromkeys(hops):
-                    lst = jobs.setdefault(h, [])
-                    base = sum(len(b[2]) for b in lst)
-                    qs = [q for q in range(len(pair)) if hops[q] == h]
-                    lst.append(("rl%d" % k, sum(len(eng[q]) for q in qs),
-                                [(base + u, pair[q]) for u, q in enumerate(qs)], j, False))
-                    fw = _alloc(topo, h, [cores[pair[q]] for q in qs])
-                    for u, q in enumerate(qs):
-                        cnt[(pair[q], j)] = len(fw[u])
-                        est[(pair[q], j)] = t + (3.0 if kind == "F" else 2.0)
-                        tr.append((q, pair[q], h, eng[q], "rl%d" % k, base + u))
-                out.append((kind, pair[0], sorted(tr)))
-            steps[j] = out
-    return steps, jobs, cnt, est
+                half = len(stay) // 2
+                for q, r in enumerate(pair):
+                    h = mine[q % len(mine)]
+                    es = stay[q * half:(q + 1) * half]
+                    hoff, _hs = eng(h)
+                    tr.append((h, es, "rx%d" % u, "relay", u, 1, 2 * u + q))
+                    jobs.setdefault(h, []).append(("R", j, len(es), [(u, r, hoff)], "rx%d" % u))
+                    cnt[(r, j)] = len(hoff)
+                    est[(r, j)] = ready + ON + OFF
+                pu.append((kind, pair[0], tr))
+            else:
+                m = am[b]
+                k = nf.get((m, d), 0)
+                nf[(m, d)] = k + 1
+                via = owners(m, d)
+                h = via[k % len(via)]
+                hoff, _hs = eng(h)
+                half = len(hoff) // 2
+                pu.append((kind, pair[0], [(h, off, "rl%d" % j, "relay", 0, 2, 2 * u)]))
+                jobs.setdefault(h, []).append(("R", j, len(off), [(0, pair[0], hoff[:half]), (1, pair[1], hoff[half:])],
+                                               "rl%d" % j))
+                for r in pair:
+                    cnt[(r, j)] = half
+                    est[(r, j)] = max(ready, L + 3.5) + OFF + OFF
+        src[j] = (pb, pc, pu)
+    for h in jobs:
+        jobs[h].sort(key=lambda job: job[0] != "R")
+    return src, jobs, cnt, est
 
 
 def _send(g, topo, trs, local_sem):
@@ -154,98 +166,89 @@ def _send(g, topo, trs, local_sem):
     return sum(len(t[1]) for t in trs)
 
 
-def _col(s):
-    return slice(s * HC, (s + 1) * HC)
+def _col(s, n=1):
+    return slice(s * HC, (s + n) * HC)
 
 
-def _halves(j):
-    return (slice(HC, TK), slice(0, HC)) if j % 2 == 0 else (slice(0, HC), slice(HC, TK))
+def _half(g, T, bank, lhs, rhs, j, h, outs):
+    ps = T["ps%d" % bank]
+    g.tensor.matmul(ps[:, 0:HC], lhs, rhs, True, True).then_inc(T.sem["mm%d" % bank], 1)
+    g.vector.wait_ge(T.sem["mm%d" % bank], 1)
+    p0 = 0 if h == (1 if j % 2 == 0 else 0) else FB
+    for q, buf, slot, sem in outs:
+        g.vector.tensor_copy(buf[p0:p0 + FB, _col(slot)], ps[q * FB:(q + 1) * FB, 0:HC]).then_inc(sem, 1)
 
 
-def _unload(g, T, ps, q, j, out, cols, sem):
-    top, bot = _halves(j)
-    rows = slice(q * FB, (q + 1) * FB)
-    g.vector.tensor_copy(out[0:FB, cols], ps[rows, top]).then_inc(sem, 1)
-    g.vector.tensor_copy(out[FB:2 * FB, cols], ps[rows, bot]).then_inc(sem, 1)
+def _helper(g, core, T, topo, jobs):
+    total = 0
+    for job in jobs:
+        j = job[1]
+        if job[0] == "R":
+            g.wait_ge(T.sem[job[4]], job[2])
+            total += _send(g, topo, [(T.cores[r], es, T.sem["arr%d" % j], T.land[:, _col(j)], T.relay[:, _col(s)])
+                                     for s, r, es in job[3]], T.sem.sent)
+            continue
+        _kind, _j, waits, lay, us = job
+        xo, wo = LAYOUT[lay]
+        for h in range(2):
+            if waits[h] is not None:
+                g.tensor.wait_ge(T.sem[waits[h][0]], waits[h][1])
+            for u, (pair, woff, _es) in enumerate(us):
+                _half(g, T, 2 * h + u, T.bun[:, wo + woff:wo + woff + W2], T.bun[:, xo + h * HC:xo + (h + 1) * HC],
+                      j, h, [(q, T.stage, 2 * u + q, T.sem["cp%d" % u]) for q in range(2)])
+        for u, (pair, woff, es) in enumerate(us):
+            g.wait_ge(T.sem["cp%d" % u], 4)
+            total += _send(g, topo, [(T.cores[r], es[q], T.sem["arr%d" % j], T.land[:, _col(j)],
+                                      T.stage[:, _col(2 * u + q)]) for q, r in enumerate(pair)], T.sem.sent)
+    g.wait_ge(T.sem.sent, total)
 
 
 def rank_program(g, core, T, topo):
-    steps, jobs, cnt, est = _plan(T.cores, topo)
+    src, jobs, cnt, est = _plan(T.cores, topo)
     rank = T.rank_of(core)
-
     if rank is None:
-        if core not in jobs:
-            return
-        total = 0
-        for sem, count, blocks, j, computes in jobs[core]:
-            src = T.relay
-            if computes:
-                g.tensor.wait_ge(T.sem[sem], count)
-                g.tensor.matmul(T.ps0[:], T.xw[:, TK:TK + 2 * FB], T.xw[:, 0:TK], True, True).then_inc(T.sem.mm0, 1)
-                g.vector.wait_ge(T.sem.mm0, 1)
-                for s, r in blocks:
-                    _unload(g, T, T.ps0, s, j, T.stage, _col(s), T.sem.cp0)
-                g.wait_ge(T.sem.cp0, 2 * len(blocks))
-                src = T.stage
-            else:
-                g.wait_ge(T.sem[sem], count)
-            eng = _alloc(topo, core, [T.cores[r] for _s, r in blocks])
-            total += _send(g, topo, [(T.cores[r], eng[u], T.sem["arr%d" % j], T.land[:, _col(j)],
-                                      src[:, _col(s)]) for u, (s, r) in enumerate(blocks)], T.sem.sent)
-        g.wait_ge(T.sem.sent, total)
+        if core in jobs:
+            _helper(g, core, T, topo, jobs[core])
         return
+    pb, pc, pu = src[rank]
 
-    my = steps[rank]
-    mats = [s for s in my if s[0] != "C"]
-    g.sync.dma_start(T.xw[:, 0:TK], T.x[:]).then_inc(T.sem.ldx, 16)
-    taken = [mats[0][1] * FB]
-    for kind, r0, tr in my:
-        if kind == "C":
-            g.scalar.dma_start(T.xw[:, TK:TK + 2 * FB], T.w[:, r0 * FB:(r0 + 2) * FB]).then_inc(T.sem.ldc, 16)
-            taken.append(r0 * FB)
-    f0 = taken[0]
-    g.scalar.dma_start(T.ws[:, f0:f0 + 2 * FB], T.w[:, f0:f0 + 2 * FB]).then_inc(T.sem.ldw0, 16)
-    rest, a = [], 0
-    for s in sorted(taken) + [N * FB]:
-        if s > a:
-            rest.append((a, s))
-        a = s + 2 * FB
-    for u, (a, b) in enumerate(rest):
-        (g.sync if u % 2 == 0 else g.scalar).dma_start(T.ws[:, a:b], T.w[:, a:b]).then_inc(T.sem.ldw1, 16)
+    g.sync.dma_start(T.xw[:, XO:XO + TK], T.x[:]).then_inc(T.sem.ldx, 16)
+    firsts = pb[2]
+    if firsts[0] + 2 == firsts[1]:
+        parts = [(0, firsts[0] * FB, 2 * W2)]
+    else:
+        parts = [(0, firsts[0] * FB, W2), (W2, firsts[1] * FB, W2)]
+    for c, wc, n in parts:
+        g.scalar.dma_start(T.xw[:, c:c + n], T.w[:, wc:wc + n]).then_inc(T.sem.lb, 16)
+    for u, (kind, r0, tr) in enumerate(pu):
+        if u == 1:
+            g.scalar.dma_start(T.xw[:, XO + TK:XO + TK + W2], T.w[:, pc[2] * FB:pc[2] * FB + W2]).then_inc(T.sem.ldc, 16)
+        (g.sync if u % 2 == 0 else g.scalar).dma_start(T.ws[:, r0 * FB:r0 * FB + W2],
+                                                       T.w[:, r0 * FB:r0 * FB + W2]).then_inc(T.sem["lw%d" % u], 16)
 
     g.tensor.wait_ge(T.sem.ldx, 16)
-    g.tensor.wait_ge(T.sem.ldw0, 16)
-    first = True
-    for k, (kind, r0, tr) in enumerate(my):
-        if kind == "C":
-            continue
-        if not first and rest:
-            g.tensor.wait_ge(T.sem.ldw1, 16 * len(rest))
-            rest = []
-        first = False
-        g.tensor.matmul(T["ps%d" % k][:], T.ws[:, r0 * FB:(r0 + 2) * FB], T.xw[:, 0:TK], True, True).then_inc(
-            T.sem["mm%d" % k], 1)
-
-    for k, (kind, r0, tr) in enumerate(my):
-        if kind == "C":
-            continue
-        g.vector.wait_ge(T.sem["mm%d" % k], 1)
-        for q, r, hop, es, sem, slot in tr:
-            _unload(g, T, T["ps%d" % k], q, rank, T.stage, _col(2 * k + q), T.sem["cp%d" % k])
-        if kind == "own":
-            _unload(g, T, T["ps%d" % k], rank - r0, rank, T.land, _col(rank), T.sem.cps)
+    for u, (kind, r0, tr) in enumerate(pu):
+        g.tensor.wait_ge(T.sem["lw%d" % u], 16)
+        for h in range(2):
+            if kind == "own":
+                outs = [(q, T.land, rank, T.sem.cps) if r0 + q == rank else (q, T.stage, 2 * u + q, T.sem["cp%d" % u])
+                        for q in range(2)]
+            else:
+                outs = [(q, T.stage, 2 * u + q, T.sem["cp%d" % u]) for q in range(2)]
+            _half(g, T, 2 * u + h, T.ws[:, r0 * FB:r0 * FB + W2], T.xw[:, XO + h * HC:XO + (h + 1) * HC], rank, h, outs)
 
     total = 0
-    for k, (kind, r0, tr) in enumerate(my):
-        if kind == "C":
-            g.wait_ge(T.sem.ldx, 16)
-            g.wait_ge(T.sem.ldc, 16)
-            total += _send(g, topo, [(tr[0][2], tr[0][3], T.sem[tr[0][4]], T.xw[:], T.xw[:])], T.sem.sent)
-            continue
-        g.wait_ge(T.sem["cp%d" % k], 2 * len(tr))
-        total += _send(g, topo, [(hop, es, T.sem[sem],
-                                  T.land[:, _col(rank)] if slot is None else T.relay[:, _col(slot)],
-                                  T.stage[:, _col(2 * k + q)]) for q, r, hop, es, sem, slot in tr], T.sem.sent)
+    g.wait_ge(T.sem.ldx, 16)
+    g.wait_ge(T.sem.lb, 16 * len(parts))
+    cut = XO + HC
+    total += _send(g, topo, [(pb[0], pb[1], T.sem.bp0, T.bun[:, 0:cut], T.xw[:, 0:cut])], T.sem.sent)
+    total += _send(g, topo, [(pb[0], pb[1], T.sem.bp1, T.bun[:, cut:XO + TK], T.xw[:, cut:XO + TK])], T.sem.sent)
+    g.wait_ge(T.sem.ldc, 16)
+    total += _send(g, topo, [(pc[0], pc[1], T.sem.cf, T.bun[:, 0:TK + W2], T.xw[:, XO:XO + TK + W2])], T.sem.sent)
+    for u, (kind, r0, tr) in enumerate(pu):
+        g.wait_ge(T.sem["cp%d" % u], 2 if kind == "own" else 4)
+        total += _send(g, topo, [(dst, es, T.sem[sem], T[buf][:, _col(slot, n)], T.stage[:, _col(s, n)])
+                                 for dst, es, sem, buf, slot, n, s in tr], T.sem.sent)
     g.wait_ge(T.sem.sent, total)
 
     st = []

@@ -3,26 +3,27 @@ from concourse.bass import DstId, RemoteDMATransfer
 NSIM = 128
 N, FB, TK = 12, 64, 512
 HC = TK // 2
+QC = HC // 2
 W2 = 2 * FB
 XO = 2 * W2
-NB = 6
+NB = 8
 
 SCRATCH = {
     "xw": ("sbuf", [128, XO + TK + W2], "float32"),
+    "xv": ("sbuf", [128, W2 + TK + W2], "float32"),
     "ws": ("sbuf", [128, N * FB], "float32"),
     "bun": ("sbuf", [128, TK + 2 * W2], "float32"),
-    "stage": ("sbuf", [128, NB * HC], "float32"),
+    "stage": ("sbuf", [128, 6 * HC], "float32"),
     "land": ("sbuf", [128, N * HC], "float32"),
-    "relay": ("sbuf", [128, 3 * HC], "float32"),
+    "relay": ("sbuf", [128, 2 * HC], "float32"),
 }
 for _k in range(NB):
     SCRATCH["ps%d" % _k] = ("psum", [128, TK], "float32")
 
-SEMAPHORES = (["ldx", "lb", "ldc", "lw0", "lw1", "lw2", "cps", "sent", "sta", "stb", "bp0", "bp1", "cf"]
-              + ["mm%d" % k for k in range(NB)] + ["cp%d" % k for k in range(3)]
-              + ["arr%d" % j for j in range(N)] + ["rl%d" % j for j in range(N)] + ["rx%d" % u for u in range(3)])
-
-LAYOUT = ((XO, 0), (0, TK))
+SEMAPHORES = (["ldx", "lb", "ldc", "ldv", "lw0", "lw1", "lw2", "cps", "sent", "sta", "stb", "bp0", "bp1", "cf"]
+              + ["mm%d" % k for k in range(NB)] + ["cp%d_%d" % (k, s) for k in range(3) for s in range(2)]
+              + ["arr%d" % j for j in range(N)] + ["rl%d_%d" % (j, s) for j in range(N) for s in range(2)]
+              + ["rx%d" % s for s in range(2)])
 
 
 def _bits(m):
@@ -61,7 +62,8 @@ def _plan(cores, topo):
         a, d = topo.chip(cj), topo.die(cj)
         off, stay = eng(cj)
         mine = owners(a, d)
-        bund, cst, units = [], None, []
+        lone = gm[a] is None
+        bund, cst, units, comp = [], None, [], []
         for b in chips:
             if b == a:
                 continue
@@ -72,58 +74,84 @@ def _plan(cores, topo):
                 units.insert(0, ("X", b))
             elif topo.same_plane(a, b):
                 cst = b
-            elif gm[a] is None:
-                units.append(("X", b))
+            elif lone:
+                comp.append(b)
             else:
                 units.append(("F", b))
-        for t in bund[1:]:
-            cst = t
-            units.insert(0, ("X", gm[t]))
+        if lone:
+            cst = bund[1]
+            comp.insert(0, gm[bund[1]])
+            units.insert(0, ("D", bund[0]))
         units.append(("own", a))
 
         t = bund[0]
-        if gm[a] is None:
+        if lone:
             idle = [c for c in allchips if topo.same_plane(a, c) and c not in chips
                     and not any(topo.mates(c, o) for o in chips)][0]
             h = owners(idle, d)[0]
             hoff, hstay = eng(h)
-            ways = ((gm[t], hoff, OFF), (t, hoff, OFF + 2.0))
+            ways = ((gm[t], hoff, OFF + 0.5),)
+            two = [gm[t]]
         else:
             k = nb.get((t, d), 0)
             nb[(t, d)] = k + 1
             h = owners(t, d)[k]
             hoff, hstay = eng(h)
             ways = ((gm[t], hoff, OFF), (t, hstay, ON))
-        two = sorted((t, gm[t]), key=lambda ch: on[ch][0])
+            two = sorted((t, gm[t]), key=lambda ch: on[ch][0])
+        s0 = XO - len(two) * W2
         us = []
         for u, (ch, ee, hop) in enumerate(ways):
             half = len(ee) // 2
             us.append((on[ch], two.index(ch) * W2, [ee[:half], ee[half:]]))
             for r in on[ch]:
-                cnt[(r, j)] = half
-                est[(r, j)] = L + OFF + 1.5 + (u + 1) * MM / 2 + CP + hop
-        jobs.setdefault(h, []).append(("K", j, [("bp0", len(off)), ("bp1", len(off))], 0, us))
-        pb = (h, off, [on[ch][0] for ch in two])
+                cnt[(r, j)] = 2 * half
+                est[(r, j)] = L + OFF + 0.5 + 0.5 * len(two) + (u + 1) * MM / 2 + CP + hop
+        jobs.setdefault(h, []).append(("K", j, [("bp0", 2 * len(off)), ("bp1", len(off))], (XO - s0, 0), us))
+        pb = (h, off, [on[ch][0] for ch in two], s0)
 
         h = [c for c in free(a, d) if c not in mine][0]
         hoff, _hs = eng(h)
         half = len(hoff) // 2
-        jobs.setdefault(h, []).append(("K", j, [("cf", len(stay)), None], 1, [(on[cst], 0, [hoff[:half], hoff[half:]])]))
+        ces = off if lone else stay
+        jobs.setdefault(h, []).append(("K", j, [("cf", len(ces)), None], (0, TK),
+                                       [(on[cst], 0, [hoff[:half], hoff[half:]])]))
         for r in on[cst]:
-            cnt[(r, j)] = half
-            est[(r, j)] = L + ON + MM + CP + OFF
-        pc = (h, stay, on[cst][0])
+            cnt[(r, j)] = 2 * half
+            est[(r, j)] = L + ON + MM + CP + OFF + (1.0 if lone else 0.0)
+        pc = (h, ces, on[cst][0])
+
+        pv = []
+        for q, b in enumerate(comp):
+            h = mine[q]
+            hoff, _hs = eng(h)
+            half = len(hoff) // 2
+            es = stay[q * (len(stay) // 2):(q + 1) * (len(stay) // 2)]
+            jobs.setdefault(h, []).append(("K", j, [("cf", len(es)), None], ((W2, 0), (0, TK))[q],
+                                           [(on[b], 0, [hoff[:half], hoff[half:]])]))
+            for r in on[b]:
+                cnt[(r, j)] = 2 * half
+                est[(r, j)] = L + 0.5 + ON + MM + CP + OFF + 0.5
+            pv.append((h, es, on[b][0], q * W2, q * (W2 + TK)))
 
         pu = []
+        arr = ("arr%d" % j, "arr%d" % j)
         for u, (kind, b) in enumerate(units):
             ready = L + (u + 1) * MM + CP
             pair = on[b]
             if kind == "own":
                 sib = [r for r in pair if r != j][0]
-                pu.append((kind, pair[0], [(cores[sib], stay, "arr%d" % j, "land", j, 1, 2 * u + pair.index(sib))]))
-                cnt[(sib, j)] = len(stay)
+                pu.append((kind, pair[0], [(cores[sib], stay, arr, "land", j * HC, QC, QC, pair.index(sib))]))
+                cnt[(sib, j)] = 2 * len(stay)
                 est[(sib, j)] = ready + ON
                 est[(j, j)] = ready
+            elif kind == "D":
+                half = len(off) // 2
+                pu.append((kind, pair[0], [(cores[r], off[q * half:(q + 1) * half], arr, "land", j * HC, QC, QC, q)
+                                           for q, r in enumerate(pair)]))
+                for r in pair:
+                    cnt[(r, j)] = 2 * half
+                    est[(r, j)] = max(ready, L + 3.5) + OFF
             elif kind == "X":
                 tr = []
                 half = len(stay) // 2
@@ -131,9 +159,9 @@ def _plan(cores, topo):
                     h = mine[q % len(mine)]
                     es = stay[q * half:(q + 1) * half]
                     hoff, _hs = eng(h)
-                    tr.append((h, es, "rx%d" % u, "relay", u, 1, 2 * u + q))
-                    jobs.setdefault(h, []).append(("R", j, len(es), [(u, r, hoff)], "rx%d" % u))
-                    cnt[(r, j)] = len(hoff)
+                    tr.append((h, es, ("rx0", "rx1"), "relay", 0, QC, QC, q))
+                    jobs.setdefault(h, []).append(("R", j, len(es), [(0, QC, r, hoff)], ("rx0", "rx1")))
+                    cnt[(r, j)] = 2 * len(hoff)
                     est[(r, j)] = ready + ON + OFF
                 pu.append((kind, pair[0], tr))
             else:
@@ -144,13 +172,14 @@ def _plan(cores, topo):
                 h = via[k % len(via)]
                 hoff, _hs = eng(h)
                 half = len(hoff) // 2
-                pu.append((kind, pair[0], [(h, off, "rl%d" % j, "relay", 0, 2, 2 * u)]))
-                jobs.setdefault(h, []).append(("R", j, len(off), [(0, pair[0], hoff[:half]), (1, pair[1], hoff[half:])],
-                                               "rl%d" % j))
+                sems = ("rl%d_0" % j, "rl%d_1" % j)
+                pu.append((kind, pair[0], [(h, off, sems, "relay", 0, HC, HC, 0)]))
+                jobs.setdefault(h, []).append(("R", j, len(off), [(0, HC, pair[0], hoff[:half]),
+                                                                  (QC, HC, pair[1], hoff[half:])], sems))
                 for r in pair:
-                    cnt[(r, j)] = half
+                    cnt[(r, j)] = 2 * half
                     est[(r, j)] = max(ready, L + 3.5) + OFF + OFF
-        src[j] = (pb, pc, pu)
+        src[j] = (pb, pc, pu, pv)
     for h in jobs:
         jobs[h].sort(key=lambda job: job[0] != "R")
     return src, jobs, cnt, est
@@ -166,17 +195,21 @@ def _send(g, topo, trs, local_sem):
     return sum(len(t[1]) for t in trs)
 
 
-def _col(s, n=1):
-    return slice(s * HC, (s + n) * HC)
+def _stg(u, s, q):
+    return 2 * u * HC + s * HC + q * QC
 
 
-def _half(g, T, bank, lhs, rhs, j, h, outs):
+def _quarters(g, T, bank, lhs, xbuf, xo, j, hs, s, outs):
     ps = T["ps%d" % bank]
-    g.tensor.matmul(ps[:, 0:HC], lhs, rhs, True, True).then_inc(T.sem["mm%d" % bank], 1)
-    g.vector.wait_ge(T.sem["mm%d" % bank], 1)
-    p0 = 0 if h == (1 if j % 2 == 0 else 0) else FB
-    for q, buf, slot, sem in outs:
-        g.vector.tensor_copy(buf[p0:p0 + FB, _col(slot)], ps[q * FB:(q + 1) * FB, 0:HC]).then_inc(sem, 1)
+    for k, h in enumerate(hs):
+        c = xo + h * HC + s * QC
+        g.tensor.matmul(ps[:, k * QC:(k + 1) * QC], lhs, xbuf[:, c:c + QC], True, True).then_inc(T.sem["mm%d" % bank], 1)
+    g.vector.wait_ge(T.sem["mm%d" % bank], len(hs))
+    for k, h in enumerate(hs):
+        p0 = 0 if h == (1 if j % 2 == 0 else 0) else FB
+        for q, buf, col, sem in outs:
+            g.vector.tensor_copy(buf[p0:p0 + FB, col:col + QC],
+                                 ps[q * FB:(q + 1) * FB, k * QC:(k + 1) * QC]).then_inc(sem, 1)
 
 
 def _helper(g, core, T, topo, jobs):
@@ -184,22 +217,33 @@ def _helper(g, core, T, topo, jobs):
     for job in jobs:
         j = job[1]
         if job[0] == "R":
-            g.wait_ge(T.sem[job[4]], job[2])
-            total += _send(g, topo, [(T.cores[r], es, T.sem["arr%d" % j], T.land[:, _col(j)], T.relay[:, _col(s)])
-                                     for s, r, es in job[3]], T.sem.sent)
+            for s in range(2):
+                g.wait_ge(T.sem[job[4][s]], job[2])
+                total += _send(g, topo, [(T.cores[r], es, T.sem["arr%d" % j],
+                                          T.land[:, j * HC + s * QC:j * HC + (s + 1) * QC],
+                                          T.relay[:, c + s * st:c + s * st + QC]) for c, st, r, es in job[3]], T.sem.sent)
             continue
-        _kind, _j, waits, lay, us = job
-        xo, wo = LAYOUT[lay]
-        for h in range(2):
-            if waits[h] is not None:
-                g.tensor.wait_ge(T.sem[waits[h][0]], waits[h][1])
+        _kind, _j, waits, (xo, wo), us = job
+        g.tensor.wait_ge(T.sem[waits[0][0]], waits[0][1])
+        if waits[1] is None:
+            seq = [((0, 1), 0), ((0, 1), 1)]
+        else:
+            seq = [((0,), 0), ((0,), 1), ((1,), 0), ((1,), 1)]
+        bank = 0
+        for i, (hs, s) in enumerate(seq):
+            if i == 2:
+                g.tensor.wait_ge(T.sem[waits[1][0]], waits[1][1])
             for u, (pair, woff, _es) in enumerate(us):
-                _half(g, T, 2 * h + u, T.bun[:, wo + woff:wo + woff + W2], T.bun[:, xo + h * HC:xo + (h + 1) * HC],
-                      j, h, [(q, T.stage, 2 * u + q, T.sem["cp%d" % u]) for q in range(2)])
-        for u, (pair, woff, es) in enumerate(us):
-            g.wait_ge(T.sem["cp%d" % u], 4)
-            total += _send(g, topo, [(T.cores[r], es[q], T.sem["arr%d" % j], T.land[:, _col(j)],
-                                      T.stage[:, _col(2 * u + q)]) for q, r in enumerate(pair)], T.sem.sent)
+                _quarters(g, T, bank, T.bun[:, wo + woff:wo + woff + W2], T.bun, xo, j, hs, s,
+                          [(q, T.stage, _stg(u, s, q), T.sem["cp%d_%d" % (u, s)]) for q in range(2)])
+                bank += 1
+        for s in range(2):
+            for u, (pair, woff, es) in enumerate(us):
+                g.wait_ge(T.sem["cp%d_%d" % (u, s)], 4)
+                total += _send(g, topo, [(T.cores[r], es[q], T.sem["arr%d" % j],
+                                          T.land[:, j * HC + s * QC:j * HC + (s + 1) * QC],
+                                          T.stage[:, _stg(u, s, q):_stg(u, s, q) + QC]) for q, r in enumerate(pair)],
+                               T.sem.sent)
     g.wait_ge(T.sem.sent, total)
 
 
@@ -210,45 +254,54 @@ def rank_program(g, core, T, topo):
         if core in jobs:
             _helper(g, core, T, topo, jobs[core])
         return
-    pb, pc, pu = src[rank]
+    pb, pc, pu, pv = src[rank]
 
-    g.sync.dma_start(T.xw[:, XO:XO + TK], T.x[:]).then_inc(T.sem.ldx, 16)
-    firsts = pb[2]
-    if firsts[0] + 2 == firsts[1]:
-        parts = [(0, firsts[0] * FB, 2 * W2)]
+    firsts, s0 = pb[2], pb[3]
+    if len(firsts) == 2 and firsts[0] + 2 == firsts[1]:
+        parts = [(s0, firsts[0] * FB, 2 * W2)]
     else:
-        parts = [(0, firsts[0] * FB, W2), (W2, firsts[1] * FB, W2)]
+        parts = [(s0 + k * W2, f * FB, W2) for k, f in enumerate(firsts)]
     for c, wc, n in parts:
-        g.scalar.dma_start(T.xw[:, c:c + n], T.w[:, wc:wc + n]).then_inc(T.sem.lb, 16)
+        g.sync.dma_start(T.xw[:, c:c + n], T.w[:, wc:wc + n]).then_inc(T.sem.lb, 16)
+    g.sync.dma_start(T.xw[:, XO:XO + TK], T.x[:]).then_inc(T.sem.ldx, 16)
     for u, (kind, r0, tr) in enumerate(pu):
         if u == 1:
+            if pv:
+                g.sync.dma_start(T.xv[:, W2:W2 + TK], T.x[:]).then_inc(T.sem.ldv, 16)
+            for _h, _es, f, _c, tc in pv:
+                g.scalar.dma_start(T.xv[:, tc:tc + W2], T.w[:, f * FB:f * FB + W2]).then_inc(T.sem.ldv, 16)
             g.scalar.dma_start(T.xw[:, XO + TK:XO + TK + W2], T.w[:, pc[2] * FB:pc[2] * FB + W2]).then_inc(T.sem.ldc, 16)
-        (g.sync if u % 2 == 0 else g.scalar).dma_start(T.ws[:, r0 * FB:r0 * FB + W2],
-                                                       T.w[:, r0 * FB:r0 * FB + W2]).then_inc(T.sem["lw%d" % u], 16)
+        (g.scalar if u < 2 else g.sync).dma_start(T.ws[:, r0 * FB:r0 * FB + W2],
+                                                  T.w[:, r0 * FB:r0 * FB + W2]).then_inc(T.sem["lw%d" % u], 16)
 
     g.tensor.wait_ge(T.sem.ldx, 16)
     for u, (kind, r0, tr) in enumerate(pu):
         g.tensor.wait_ge(T.sem["lw%d" % u], 16)
-        for h in range(2):
-            if kind == "own":
-                outs = [(q, T.land, rank, T.sem.cps) if r0 + q == rank else (q, T.stage, 2 * u + q, T.sem["cp%d" % u])
-                        for q in range(2)]
-            else:
-                outs = [(q, T.stage, 2 * u + q, T.sem["cp%d" % u]) for q in range(2)]
-            _half(g, T, 2 * u + h, T.ws[:, r0 * FB:r0 * FB + W2], T.xw[:, XO + h * HC:XO + (h + 1) * HC], rank, h, outs)
+        for s in range(2):
+            outs = [(q, T.land, rank * HC + s * QC, T.sem.cps) if kind == "own" and r0 + q == rank
+                    else (q, T.stage, _stg(u, s, q), T.sem["cp%d_%d" % (u, s)]) for q in range(2)]
+            _quarters(g, T, 2 * u + s, T.ws[:, r0 * FB:r0 * FB + W2], T.xw, XO, rank, (0, 1), s, outs)
 
     total = 0
-    g.wait_ge(T.sem.ldx, 16)
     g.wait_ge(T.sem.lb, 16 * len(parts))
     cut = XO + HC
-    total += _send(g, topo, [(pb[0], pb[1], T.sem.bp0, T.bun[:, 0:cut], T.xw[:, 0:cut])], T.sem.sent)
-    total += _send(g, topo, [(pb[0], pb[1], T.sem.bp1, T.bun[:, cut:XO + TK], T.xw[:, cut:XO + TK])], T.sem.sent)
+    total += _send(g, topo, [(pb[0], pb[1], T.sem.bp0, T.bun[:, 0:XO - s0], T.xw[:, s0:XO])], T.sem.sent)
+    g.wait_ge(T.sem.ldx, 16)
+    total += _send(g, topo, [(pb[0], pb[1], T.sem.bp0, T.bun[:, XO - s0:cut - s0], T.xw[:, XO:cut])], T.sem.sent)
+    total += _send(g, topo, [(pb[0], pb[1], T.sem.bp1, T.bun[:, cut - s0:XO + TK - s0], T.xw[:, cut:XO + TK])],
+                   T.sem.sent)
+    if pv:
+        g.wait_ge(T.sem.ldv, 16 * (1 + len(pv)))
+        total += _send(g, topo, [(h, es, T.sem.cf, T.bun[:, 0:TK + W2], T.xv[:, c:c + TK + W2])
+                                 for h, es, _f, c, _tc in pv], T.sem.sent)
     g.wait_ge(T.sem.ldc, 16)
     total += _send(g, topo, [(pc[0], pc[1], T.sem.cf, T.bun[:, 0:TK + W2], T.xw[:, XO:XO + TK + W2])], T.sem.sent)
     for u, (kind, r0, tr) in enumerate(pu):
-        g.wait_ge(T.sem["cp%d" % u], 2 if kind == "own" else 4)
-        total += _send(g, topo, [(dst, es, T.sem[sem], T[buf][:, _col(slot, n)], T.stage[:, _col(s, n)])
-                                 for dst, es, sem, buf, slot, n, s in tr], T.sem.sent)
+        for s in range(2):
+            g.wait_ge(T.sem["cp%d_%d" % (u, s)], 2 if kind == "own" else 4)
+            total += _send(g, topo, [(dst, es, T.sem[sems[s]], T[buf][:, dc + s * st:dc + s * st + n],
+                                      T.stage[:, _stg(u, s, q):_stg(u, s, q) + n])
+                                     for dst, es, sems, buf, dc, st, n, q in tr], T.sem.sent)
     g.wait_ge(T.sem.sent, total)
 
     st = []
@@ -264,7 +317,7 @@ def rank_program(g, core, T, topo):
         qu, sem = ((g.sync, T.sem.sta), (g.scalar, T.sem.stb))[u % 2]
         for j in range(slot, slot + ns):
             if j == rank:
-                qu.wait_ge(T.sem.cps, 2)
+                qu.wait_ge(T.sem.cps, 4)
             else:
                 qu.wait_ge(T.sem["arr%d" % j], cnt[(rank, j)])
         qu.dma_start(T.y[:, col:col + ns * HC], T.land[p0:p0 + FB, slot * HC:(slot + ns) * HC]).then_inc(sem, 16)

from concourse.bass import DstId, RemoteDMATransfer

NSIM = 128
N, FB, TK = 12, 64, 512
HC = TK // 2
QC = HC // 2
W2 = 2 * FB
XO = 2 * W2
NB = 8

SCRATCH = {
    "xw": ("sbuf", [128, XO + TK + W2], "float32"),
    "xv": ("sbuf", [128, W2 + TK + W2], "float32"),
    "ws": ("sbuf", [128, N * FB], "float32"),
    "bun": ("sbuf", [128, TK + 2 * W2], "float32"),
    "stage": ("sbuf", [128, 6 * HC], "float32"),
    "land": ("sbuf", [128, N * HC], "float32"),
    "relay": ("sbuf", [128, 2 * HC], "float32"),
}
for _k in range(NB):
    SCRATCH["ps%d" % _k] = ("psum", [128, TK], "float32")

SEMAPHORES = (["ldx", "lb", "ldc", "ldv", "lw0", "lw1", "lw2", "cps", "sent", "sta", "stb", "bp0", "bp1", "cf"]
              + ["mm%d" % k for k in range(NB)] + ["cp%d_%d" % (k, s) for k in range(3) for s in range(2)]
              + ["arr%d" % j for j in range(N)] + ["rl%d_%d" % (j, s) for j in range(N) for s in range(2)]
              + ["rx%d" % s for s in range(2)])


def _bits(m):
    return [e for e in range(m.bit_length()) if (m >> e) & 1]


def _mask(es):
    m = 0
    for e in es:
        m |= 1 << e
    return m


def _plan(cores, topo):
    allchips = sorted({topo.chip(c) for c in range(NSIM)})
    chips = list(dict.fromkeys(topo.chip(c) for c in cores))
    on = {ch: [r for r, c in enumerate(cores) if topo.chip(c) == ch] for ch in chips}
    gm = {ch: ([o for o in chips if topo.mates(ch, o)] or [None])[0] for ch in chips}
    am = {ch: [o for o in allchips if topo.mates(ch, o)][0] for ch in chips}

    def free(ch, d):
        return [c for c in range(NSIM) if topo.chip(c) == ch and topo.die(c) == d and c not in cores]

    def owners(ch, d):
        return [c for c in free(ch, d) if all(topo.may_write(c, t) for t in cores)]

    def eng(c):
        near = [o for o in range(NSIM) if o != c and topo.chip(o) == topo.chip(c)][0]
        far = [o for o in range(NSIM) if topo.chip(o) != topo.chip(c)][0]
        of = _bits(topo.mask(c, far))
        return of, [e for e in _bits(topo.mask(c, near)) if e not in of]

    L, MM, CP, ON, OFF = 2.2, 1.9, 0.5, 2.3, 3.0
    src, jobs, cnt, est, nb, nf = {}, {}, {}, {}, {}, {}
    for j, cj in enumerate(cores):
        a, d = topo.chip(cj), topo.die(cj)
        off, stay = eng(cj)
        mine = owners(a, d)
        lone = gm[a] is None
        bund, cst, units, comp = [], None, [], []
        for b in chips:
            if b == a:
                continue
            if gm[b] is not None and gm[b] != a:
                if topo.same_plane(a, b):
                    bund.append(b)
            elif gm[b] == a:
                units.insert(0, ("X", b))
            elif topo.same_plane(a, b):
                cst = b
            elif lone:
                comp.append(b)
            else:
                units.append(("F", b))
        if lone:
            cst = bund[1]
            comp.insert(0, gm[bund[1]])
            units.insert(0, ("D", bund[0]))
        units.append(("own", a))

        t = bund[0]
        if lone:
            idle = [c for c in allchips if topo.same_plane(a, c) and c not in chips
                    and not any(topo.mates(c, o) for o in chips)][0]
            h = owners(idle, d)[0]
            hoff, hstay = eng(h)
            ways = ((gm[t], hoff, OFF + 0.5),)
            two = [gm[t]]
        else:
            k = nb.get((t, d), 0)
            nb[(t, d)] = k + 1
            h = owners(t, d)[k]
            hoff, hstay = eng(h)
            ways = ((gm[t], hoff, OFF), (t, hstay, ON))
            two = sorted((t, gm[t]), key=lambda ch: on[ch][0])
        s0 = XO - len(two) * W2
        us = []
        for u, (ch, ee, hop) in enumerate(ways):
            half = len(ee) // 2
            us.append((on[ch], two.index(ch) * W2, [ee[:half], ee[half:]]))
            for r in on[ch]:
                cnt[(r, j)] = 2 * half
                est[(r, j)] = L + OFF + 0.5 + 0.5 * len(two) + (u + 1) * MM / 2 + CP + hop
        jobs.setdefault(h, []).append(("K", j, [("bp0", 2 * len(off)), ("bp1", len(off))], (XO - s0, 0), us))
        pb = (h, off, [on[ch][0] for ch in two], s0)

        h = [c for c in free(a, d) if c not in mine][0]
        hoff, _hs = eng(h)
        half = len(hoff) // 2
        ces = off if lone else stay
        jobs.setdefault(h, []).append(("K", j, [("cf", len(ces)), None], (0, TK),
                                       [(on[cst], 0, [hoff[:half], hoff[half:]])]))
        for r in on[cst]:
            cnt[(r, j)] = 2 * half
            est[(r, j)] = L + ON + MM + CP + OFF + (1.0 if lone else 0.0)
        pc = (h, ces, on[cst][0])

        pv = []
        for q, b in enumerate(comp):
            h = mine[q]
            hoff, _hs = eng(h)
            half = len(hoff) // 2
            es = stay[q * (len(stay) // 2):(q + 1) * (len(stay) // 2)]
            jobs.setdefault(h, []).append(("K", j, [("cf", len(es)), None], ((W2, 0), (0, TK))[q],
                                           [(on[b], 0, [hoff[:half], hoff[half:]])]))
            for r in on[b]:
                cnt[(r, j)] = 2 * half
                est[(r, j)] = L + 0.5 + ON + MM + CP + OFF + 0.5
            pv.append((h, es, on[b][0], q * W2, q * (W2 + TK)))

        pu = []
        arr = ("arr%d" % j, "arr%d" % j)
        for u, (kind, b) in enumerate(units):
            ready = L + (u + 1) * MM + CP
            pair = on[b]
            if kind == "own":
                sib = [r for r in pair if r != j][0]
                pu.append((kind, pair[0], [(cores[sib], stay, arr, "land", j * HC, QC, QC, pair.index(sib))]))
                cnt[(sib, j)] = 2 * len(stay)
                est[(sib, j)] = ready + ON
                est[(j, j)] = ready
            elif kind == "D":
                half = len(off) // 2
                pu.append((kind, pair[0], [(cores[r], off[q * half:(q + 1) * half], arr, "land", j * HC, QC, QC, q)
                                           for q, r in enumerate(pair)]))
                for r in pair:
                    cnt[(r, j)] = 2 * half
                    est[(r, j)] = max(ready, L + 3.5) + OFF
            elif kind == "X":
                tr = []
                half = len(stay) // 2
                for q, r in enumerate(pair):
                    h = mine[q % len(mine)]
                    es = stay[q * half:(q + 1) * half]
                    hoff, _hs = eng(h)
                    tr.append((h, es, ("rx0", "rx1"), "relay", 0, QC, QC, q))
                    jobs.setdefault(h, []).append(("R", j, len(es), [(0, QC, r, hoff)], ("rx0", "rx1")))
                    cnt[(r, j)] = 2 * len(hoff)
                    est[(r, j)] = ready + ON + OFF
                pu.append((kind, pair[0], tr))
            else:
                m = am[b]
                k = nf.get((m, d), 0)
                nf[(m, d)] = k + 1
                via = owners(m, d)
                h = via[k % len(via)]
                hoff, _hs = eng(h)
                half = len(hoff) // 2
                sems = ("rl%d_0" % j, "rl%d_1" % j)
                pu.append((kind, pair[0], [(h, off, sems, "relay", 0, HC, HC, 0)]))
                jobs.setdefault(h, []).append(("R", j, len(off), [(0, HC, pair[0], hoff[:half]),
                                                                  (QC, HC, pair[1], hoff[half:])], sems))
                for r in pair:
                    cnt[(r, j)] = 2 * half
                    est[(r, j)] = max(ready, L + 3.5) + OFF + OFF
        src[j] = (pb, pc, pu, pv)
    for h in jobs:
        jobs[h].sort(key=lambda job: job[0] != "R")
    return src, jobs, cnt, est


def _send(g, topo, trs, local_sem):
    lst = []
    for dst, es, sem, out_ap, in_ap in trs:
        rid, pid, _se = topo.addr(dst)
        lst.append(RemoteDMATransfer(dst_ids=[DstId(rid=rid, pnc=pid)], dma_engine_mask=_mask(es), remote_sem=sem,
                                     src=in_ap, dst=out_ap))
    g.remote_dma_fused(lst, local_sem=local_sem)
    return sum(len(t[1]) for t in trs)


def _stg(u, s, q):
    return 2 * u * HC + s * HC + q * QC


def _quarters(g, T, bank, lhs, xbuf, xo, j, hs, s, outs):
    ps = T["ps%d" % bank]
    for k, h in enumerate(hs):
        c = xo + h * HC + s * QC
        g.tensor.matmul(ps[:, k * QC:(k + 1) * QC], lhs, xbuf[:, c:c + QC], True, True).then_inc(T.sem["mm%d" % bank], 1)
    g.vector.wait_ge(T.sem["mm%d" % bank], len(hs))
    for k, h in enumerate(hs):
        p0 = 0 if h == (1 if j % 2 == 0 else 0) else FB
        for q, buf, col, sem in outs:
            g.vector.tensor_copy(buf[p0:p0 + FB, col:col + QC],
                                 ps[q * FB:(q + 1) * FB, k * QC:(k + 1) * QC]).then_inc(sem, 1)


def _helper(g, core, T, topo, jobs):
    total = 0
    for job in jobs:
        j = job[1]
        if job[0] == "R":
            for s in range(2):
                g.wait_ge(T.sem[job[4][s]], job[2])
                total += _send(g, topo, [(T.cores[r], es, T.sem["arr%d" % j],
                                          T.land[:, j * HC + s * QC:j * HC + (s + 1) * QC],
                                          T.relay[:, c + s * st:c + s * st + QC]) for c, st, r, es in job[3]], T.sem.sent)
            continue
        _kind, _j, waits, (xo, wo), us = job
        g.tensor.wait_ge(T.sem[waits[0][0]], waits[0][1])
        if waits[1] is None:
            seq = [((0, 1), 0), ((0, 1), 1)]
        else:
            seq = [((0,), 0), ((0,), 1), ((1,), 0), ((1,), 1)]
        bank = 0
        for i, (hs, s) in enumerate(seq):
            if i == 2:
                g.tensor.wait_ge(T.sem[waits[1][0]], waits[1][1])
            for u, (pair, woff, _es) in enumerate(us):
                _quarters(g, T, bank, T.bun[:, wo + woff:wo + woff + W2], T.bun, xo, j, hs, s,
                          [(q, T.stage, _stg(u, s, q), T.sem["cp%d_%d" % (u, s)]) for q in range(2)])
                bank += 1
        for s in range(2):
            for u, (pair, woff, es) in enumerate(us):
                g.wait_ge(T.sem["cp%d_%d" % (u, s)], 4)
                total += _send(g, topo, [(T.cores[r], es[q], T.sem["arr%d" % j],
                                          T.land[:, j * HC + s * QC:j * HC + (s + 1) * QC],
                                          T.stage[:, _stg(u, s, q):_stg(u, s, q) + QC]) for q, r in enumerate(pair)],
                               T.sem.sent)
    g.wait_ge(T.sem.sent, total)


def rank_program(g, core, T, topo):
    src, jobs, cnt, est = _plan(T.cores, topo)
    rank = T.rank_of(core)
    if rank is None:
        if core in jobs:
            _helper(g, core, T, topo, jobs[core])
        return
    pb, pc, pu, pv = src[rank]

    firsts, s0 = pb[2], pb[3]
    if len(firsts) == 2 and firsts[0] + 2 == firsts[1]:
        parts = [(s0, firsts[0] * FB, 2 * W2)]
    else:
        parts = [(s0 + k * W2, f * FB, W2) for k, f in enumerate(firsts)]
    for c, wc, n in parts:
        g.sync.dma_start(T.xw[:, c:c + n], T.w[:, wc:wc + n]).then_inc(T.sem.lb, 16)
    g.sync.dma_start(T.xw[:, XO:XO + TK], T.x[:]).then_inc(T.sem.ldx, 16)
    for u, (kind, r0, tr) in enumerate(pu):
        if u == 1:
            if pv:
                g.sync.dma_start(T.xv[:, W2:W2 + TK], T.x[:]).then_inc(T.sem.ldv, 16)
            for _h, _es, f, _c, tc in pv:
                g.scalar.dma_start(T.xv[:, tc:tc + W2], T.w[:, f * FB:f * FB + W2]).then_inc(T.sem.ldv, 16)
            g.scalar.dma_start(T.xw[:, XO + TK:XO + TK + W2], T.w[:, pc[2] * FB:pc[2] * FB + W2]).then_inc(T.sem.ldc, 16)
        (g.scalar if u < 2 else g.sync).dma_start(T.ws[:, r0 * FB:r0 * FB + W2],
                                                  T.w[:, r0 * FB:r0 * FB + W2]).then_inc(T.sem["lw%d" % u], 16)

    g.tensor.wait_ge(T.sem.ldx, 16)
    for u, (kind, r0, tr) in enumerate(pu):
        g.tensor.wait_ge(T.sem["lw%d" % u], 16)
        for s in range(2):
            outs = [(q, T.land, rank * HC + s * QC, T.sem.cps) if kind == "own" and r0 + q == rank
                    else (q, T.stage, _stg(u, s, q), T.sem["cp%d_%d" % (u, s)]) for q in range(2)]
            _quarters(g, T, 2 * u + s, T.ws[:, r0 * FB:r0 * FB + W2], T.xw, XO, rank, (0, 1), s, outs)

    total = 0
    g.wait_ge(T.sem.lb, 16 * len(parts))
    cut = XO + HC
    total += _send(g, topo, [(pb[0], pb[1], T.sem.bp0, T.bun[:, 0:XO - s0], T.xw[:, s0:XO])], T.sem.sent)
    g.wait_ge(T.sem.ldx, 16)
    total += _send(g, topo, [(pb[0], pb[1], T.sem.bp0, T.bun[:, XO - s0:cut - s0], T.xw[:, XO:cut])], T.sem.sent)
    total += _send(g, topo, [(pb[0], pb[1], T.sem.bp1, T.bun[:, cut - s0:XO + TK - s0], T.xw[:, cut:XO + TK])],
                   T.sem.sent)
    if pv:
        g.wait_ge(T.sem.ldv, 16 * (1 + len(pv)))
        total += _send(g, topo, [(h, es, T.sem.cf, T.bun[:, 0:TK + W2], T.xv[:, c:c + TK + W2])
                                 for h, es, _f, c, _tc in pv], T.sem.sent)
    g.wait_ge(T.sem.ldc, 16)
    total += _send(g, topo, [(pc[0], pc[1], T.sem.cf, T.bun[:, 0:TK + W2], T.xw[:, XO:XO + TK + W2])], T.sem.sent)
    for u, (kind, r0, tr) in enumerate(pu):
        for s in range(2):
            g.wait_ge(T.sem["cp%d_%d" % (u, s)], 2 if kind == "own" else 4)
            total += _send(g, topo, [(dst, es, T.sem[sems[s]], T[buf][:, dc + s * st:dc + s * st + n],
                                      T.stage[:, _stg(u, s, q):_stg(u, s, q) + n])
                                     for dst, es, sems, buf, dc, st, n, q in tr], T.sem.sent)
    g.wait_ge(T.sem.sent, total)

    st = []
    for c in range(N // 2):
        st.append((0, 2 * c, 2, 2 * TK * c + HC))
    for c in range(N // 2 - 1):
        st.append((FB, 2 * c + 1, 2, 2 * TK * c + 3 * HC))
    st.append((FB, 0, 1, 0))
    st.append((FB, N - 1, 1, N * TK - HC))
    st.sort(key=lambda s: (max(est[(rank, j)] for j in range(s[1], s[1] + s[2])), s[1]))
    nq = [0, 0]
    for u, (p0, slot, ns, col) in enumerate(st):
        qu, sem = ((g.sync, T.sem.sta), (g.scalar, T.sem.stb))[u % 2]
        for j in range(slot, slot + ns):
            if j == rank:
                qu.wait_ge(T.sem.cps, 4)
            else:
                qu.wait_ge(T.sem["arr%d" % j], cnt[(rank, j)])
        qu.dma_start(T.y[:, col:col + ns * HC], T.land[p0:p0 + FB, slot * HC:(slot + ns) * HC]).then_inc(sem, 16)
        nq[u % 2] += 16
    g.sync.wait_ge(T.sem.sta, nq[0])
    g.scalar.wait_ge(T.sem.stb, nq[1])
